import numpy as np
import ml_dtypes


def mxq(x, axis, fmt="e4m3"):
    dtype, down = {"e4m3": (ml_dtypes.float8_e4m3fn, 7), "e5m2": (ml_dtypes.float8_e5m2, 14)}[fmt]
    v = np.moveaxis(np.asarray(x, np.float32).astype(ml_dtypes.bfloat16).astype(np.float64), axis, -1)
    blocks = v.reshape(v.shape[:-1] + (-1, 32))
    amax = np.abs(blocks).max(-1, keepdims=True)
    byte = np.maximum(np.where(amax > 0, np.frexp(amax)[1] - 1 + 127, 0) - down, 1)
    scale = np.exp2(byte - 127.0)
    codes = (blocks / scale).astype(np.float32).astype(dtype).astype(np.float64)
    return np.moveaxis((codes * scale).reshape(v.shape), -1, axis)


WIDE = False


def mx_kscale(k):
    if not WIDE:
        return np.ones(k)
    levels = np.array([10, -10, 5, -5, 0])
    if k % 512:
        return np.exp2(np.random.permutation(np.resize(levels, k // 32))).repeat(32)
    a = np.empty((k // 512, 16))
    for p in range(k // 512):
        a[p, :8] = np.random.permutation(np.resize(levels, 8))
        for g in range(8):
            far = levels[np.abs(levels - a[p, g]) >= 10]
            a[p, g + 8] = far[np.random.randint(len(far))]
    return np.exp2(a.ravel()).repeat(32)


BF16 = ml_dtypes.bfloat16


def bf(x):
    return np.asarray(x, np.float32).astype(BF16)


def f64(x):
    return np.asarray(x).astype(np.float64)


E2M1 = np.array([0.0, 0.5, 1.0, 1.5, 2.0, 3.0, 4.0, 6.0, -0.0, -0.5, -1.0, -1.5, -2.0, -3.0, -4.0, -6.0])


def pack_weight(w, fmt):
    k, n = w.shape
    w = f64(bf(w)).reshape(k // 32, 32, n)
    amax = np.abs(w).max(1)
    if fmt == "e4m3":
        byte = np.frexp(amax)[1] - 1 + 127 - 7
    else:
        mant, ex = np.frexp(amax / 6.0)
        byte = np.where(mant > 0.5, ex, ex - 1) + 127
    byte = np.clip(np.where(amax > 0, byte, 1), 1, 254)
    scaled = (w * np.exp2(127.0 - byte)[:, None, :]).reshape(k, n).astype(np.float32)
    by_word = np.ascontiguousarray(scaled.reshape(k // 512, 128, 4, n).transpose(0, 1, 3, 2))
    if fmt == "e4m3":
        words = by_word.astype(ml_dtypes.float8_e4m3fn).view(np.uint8)
    else:
        c = by_word.astype(ml_dtypes.float4_e2m1fn).view(np.uint8) & 0xF
        words = c[..., 0::2] | (c[..., 1::2] << 4)
    return np.ascontiguousarray(words), np.ascontiguousarray(byte.astype(np.uint8).reshape(k // 512, 16, n))


def unpack_weight(words, scales, fmt):
    g, p, n, _ = words.shape
    if fmt == "e4m3":
        vals = np.ascontiguousarray(words).view(ml_dtypes.float8_e4m3fn).astype(np.float64)
    else:
        nib = np.empty((g, p, n, 4), np.uint8)
        nib[..., 0::2] = words & 0xF
        nib[..., 1::2] = words >> 4
        vals = E2M1[nib]
    vals = vals * np.repeat(np.exp2(scales.astype(np.float64) - 127.0), 8, axis=1)[..., None]
    return vals.transpose(0, 1, 3, 2).reshape(g * 512, n)

def planes(Y):
    n, m = Y.shape
    b = f64(bf(Y)).reshape(n // 32, 32, m)
    amax = np.abs(b).max(1)
    byte = np.clip(np.where(amax > 0, np.frexp(amax)[1] - 1 + 127 - 7, 1), 1, 254)
    codes = (b * np.exp2(127.0 - byte)[:, None, :]).reshape(n, m).astype(np.float32).astype(ml_dtypes.float8_e4m3fn).view(np.uint8)
    words = codes.reshape(n // 512, 128, 4, m).transpose(0, 1, 3, 2)
    return np.ascontiguousarray(words), np.ascontiguousarray(byte.astype(np.uint8).reshape(n // 512, 16, m))


N, D = 2048, 1024


def scaled_score(y, rho, a):
    return rho[:, None] * a[None, :] * np.tanh(a[None, :] * y)


def setup_inputs():
    s, r = mx_kscale(D), mx_kscale(N)
    x = np.random.standard_normal((N, D)) * s[None, :] * r[:, None]
    rho = np.random.uniform(0.5, 1.5, N) / r
    w = np.random.standard_normal((D, D)) / np.sqrt(D) / s[:, None]
    a = np.random.uniform(0.5, 1.5, D)
    w_words, w_scales = pack_weight(w, "e4m3")
    return {"x": bf(x), "rho": bf(rho), "w_words": w_words, "w_scales": w_scales, "a": bf(a)}


def core(x, rho, w_words, w_scales, a):
    x, rho, a = f64(x), f64(rho), f64(a)
    w = unpack_weight(w_words, w_scales, "e4m3")
    n, d = x.shape[0], w.shape[1]
    root_n = np.sqrt(n)
    u = mxq(x, 1, "e4m3") @ w
    y = rho[:, None] * u
    f = scaled_score(y, rho, a)
    c = mxq(u, 0, "e4m3").T @ mxq(f, 0, "e4m3")
    grad = c / root_n - root_n * np.eye(d)
    return grad


def reference(x, rho, w_words, w_scales, a):
    R_out = core(x, rho, w_words, w_scales, a)
    words, scales = planes(R_out.T)
    return R_out, words, scales

from contextlib import ExitStack

import concourse.mybir as mybir
from concourse.masks import make_identity

N, D = 2048, 1024
FLOPS = 2 * (2 * N * D * D)

F32 = mybir.dt.float32
BF16 = mybir.dt.bfloat16
U32 = mybir.dt.uint32
I32 = mybir.dt.int32
U8 = mybir.dt.uint8
FP8X4 = mybir.dt.float8_e4m3fn_x4
ACT = mybir.ActivationFunctionType
ALU = mybir.AluOpType

P = 128
T = 4
PASS = P * T
NG = N // PASS
KG = D // PASS
CW = 128
NC = D // CW
ROOT_N = float(N) ** 0.5

X_LEAD = 7
RA_HEAD, RA_FIRST, RA_STEP, RA_ENGINE = 2, 1, (2, 3), "VVS"
XC_ENGINE = "SSSS"
PART_COLS = 4096


def tile_maximumlikelihoodicarelativegradient_x2_kernel(
    tc, x, rho, w_words, w_scales, a, grad, grad_words, grad_scales
):
    nc = tc.nc

    with ExitStack() as ctx:
        keep = ctx.enter_context(tc.tile_pool(name="keep", bufs=1))
        xin = ctx.enter_context(tc.tile_pool(name="xin", bufs=3))
        xgp = ctx.enter_context(tc.tile_pool(name="xgp", bufs=2))
        rp = ctx.enter_context(tc.tile_pool(name="rp", bufs=6))
        st = ctx.enter_context(tc.tile_pool(name="st", bufs=3))
        op = ctx.enter_context(tc.tile_pool(name="op", bufs=10))
        pp = ctx.enter_context(tc.tile_pool(name="pp", bufs=2))
        ps_s1 = ctx.enter_context(tc.psum_pool(name="ps_s1", bufs=3))
        ps_tr = ctx.enter_context(tc.psum_pool(name="ps_tr", bufs=2))
        ps_acc = ctx.enter_context(tc.psum_pool(name="ps_acc", bufs=3))
        ctx.enter_context(tc.manual_schedule())

        warm = keep.tile([P, 1], F32, name="warm")
        nc.vector.memset(warm[:], 0.0)
        wsc = keep.tile([P, D], U8, name="wsc", align_bytes=64)
        nc.vector.memset(wsc[:].bitcast(I32), 0)
        ident = keep.tile([P, P], F32, name="ident")
        make_identity(nc, ident[:])

        a_b = keep.tile([P, D], BF16, name="a_b")
        nc.scalar.dma_start(out=a_b[:, 0 : D // 2], in_=a[0 : D // 2].partition_broadcast(P))
        rho_b = keep.tile([P, NG, T], BF16, name="rho_b")
        nc.scalar.dma_start(out=rho_b[:], in_=rho.rearrange("(g p t) -> p g t", p=P, t=T))
        for q in range(4):
            nc.scalar.dma_start(
                out=wsc[32 * q : 32 * q + 8, :].bitcast(I32),
                in_=w_scales[:, 4 * q : 4 * q + 4, :].bitcast(I32),
            )
        nc.scalar.activation(out=warm[:], in_=warm[:], func=ACT.Tanh)

        x_rows = x.rearrange("(g p t) k -> g p t k", p=P, t=T)
        w_rows = w_words.rearrange("h p n t -> p h (n t)")
        wco = keep.tile([P, KG, D], U32, name="wco", align_bytes=64)
        xr = {}

        def load_x(g, pieces):
            xr[g] = xin.tile([P, T, D], BF16, name="xr")
            w = T // pieces
            for t in range(0, T, w):
                nc.sync.dma_start(out=xr[g][:, t : t + w, :], in_=x_rows[g][:, t : t + w, :])

        def load_w(c0, c1):
            for h in range(KG):
                nc.sync.dma_start(
                    out=wco[:, h, c0:c1].bitcast(I32), in_=w_rows[:, h, 4 * c0 : 4 * c1].bitcast(I32)
                )

        load_x(0, 4)
        load_w(0, 512)
        load_x(1, 2)
        nc.sync.dma_start(out=a_b[:, D // 2 :], in_=a[D // 2 :].partition_broadcast(P))
        load_x(2, 2)

        rho_f = keep.tile([P, NG, T], F32, name="rho_f")
        nc.vector.tensor_copy(out=rho_f[:], in_=rho_b[:])
        neg_eye = keep.tile([P, P], F32, name="neg_eye")
        ra = {}

        def make_ra(half, g, t, engine):
            if t == 0:
                ra[half, g] = rp.tile([P, T, D // 2], F32, name="ra")
            src, dst = a_b[:, D // 2 * half : D // 2 * (half + 1)], ra[half, g][:, t, :]
            if engine == "V":
                nc.vector.tensor_scalar(out=dst, in0=src, scalar1=rho_f[:, g, t : t + 1], scalar2=None, op0=ALU.mult)
            else:
                nc.scalar.activation(out=dst, in_=src, func=ACT.Copy, scale=rho_f[:, g, t : t + 1])

        xco = keep.tile([P, KG, N], U32, name="xco", align_bytes=64)
        xsc = keep.tile([P, KG, N], U8, name="xsc", align_bytes=64)
        xbank, xg = {}, {}

        def x_transpose(j):
            g, h, tp = j // 4, j % 4 // 2, j % 2
            pool, tag = (ps_tr, "tr") if j % 2 == 0 else (ps_acc, "acc")
            xbank[j] = pool.tile([P, 2, 2, P], F32, name=tag)
            for tt in range(2):
                words = xr[g][:, 2 * tp + tt, :].bitcast(F32)
                for u in range(2):
                    nc.tensor.transpose(xbank[j][:, tt, u, :], words[:, 256 * h + u : 256 * (h + 1) : 2], ident[:])

        def x_copy(j):
            g, h, tp = j // 4, j % 4 // 2, j % 2
            if j % 4 == 0:
                xg[g] = xgp.tile([P, KG, PASS, T], BF16, name="xg", align_bytes=64)
            dst = xg[g][:, h, 256 * tp : 256 * tp + 256, :].rearrange("p n t -> p (n t)").bitcast(F32)
            dst = dst.rearrange("p (a r u) -> p a r u", a=2, u=2)
            src = xbank[j][:].rearrange("p a u r -> p a r u")
            if XC_ENGINE[j % 4] == "S":
                nc.scalar.copy(out=dst, in_=src)
            else:
                nc.vector.tensor_copy(out=dst, in_=src)

        def x_quant(g, h):
            cols = slice(PASS * g, PASS * (g + 1))
            nc.vector.quantize_mx(
                out=xco[:, h, cols].bitcast(FP8X4),
                scales=xsc[:, h, cols],
                in_=xg[g][:, h, :, :].rearrange("p n t -> p (n t)"),
            )

        uco = keep.tile([P, NG, D], U32, name="uco", align_bytes=64)
        usc = keep.tile([P, NG, D], U8, name="usc", align_bytes=64)
        fco = keep.tile([P, NG, D], U32, name="fco", align_bytes=64)
        fsc = keep.tile([P, NG, D], U8, name="fsc", align_bytes=64)
        units = [(c, g) for g in range(NG) for c in range(NC // 2)]
        units += [(c, g) for c in range(NC // 2, NC) for g in range(NG)]
        last = [max(s for s, (c, g) in enumerate(units) if c == want) for want in range(NC)]
        ubank, zt, th, ub, fb = {}, {}, {}, {}, {}

        def ra_slice(s):
            c, g = units[s]
            return ra[c // 4, g][:, :, CW * (c % 4) : CW * (c % 4 + 1)]

        def s1(s):
            c, g = units[s]
            ubank[s] = ps_s1.tile([P, T, CW], F32, name="s1")
            for t in range(T):
                n0 = PASS * g + P * t
                for h in range(KG):
                    nc.tensor.matmul_mx(
                        out=ubank[s][:, t, :],
                        lhsT=xco[:, h, n0 : n0 + P].bitcast(FP8X4),
                        lhsT_scale=xsc[:, h, n0 : n0 + P],
                        rhs=wco[:, h, CW * c : CW * (c + 1)].bitcast(FP8X4),
                        rhs_scale=wsc[4 * h :, CW * c : CW * (c + 1)],
                        start=(h == 0),
                        stop=(h == KG - 1),
                    )

        def z_mul(s):
            zt[s] = st.tile([P, T, CW], F32, name="z")
            nc.vector.tensor_tensor(out=zt[s][:], in0=ubank[s][:], in1=ra_slice(s), op=ALU.mult)

        def u_copy(s):
            ub[s] = st.tile([P, CW, T], BF16, name="ub", align_bytes=64)
            nc.scalar.copy(out=ub[s][:], in_=ubank[s][:].rearrange("p t j -> p j t"))

        def tanh(s):
            th[s] = st.tile([P, T, CW], F32, name="th")
            nc.scalar.activation(out=th[s][:], in_=zt[s][:], func=ACT.Tanh)

        def f_mul(s):
            fb[s] = st.tile([P, CW, T], BF16, name="fb", align_bytes=64)
            nc.vector.tensor_tensor(
                out=fb[s][:].rearrange("p (c i) t -> p c t i", i=2),
                in0=th[s][:].rearrange("p t (c i) -> p c t i", i=2),
                in1=ra_slice(s).rearrange("p t (c i) -> p c t i", i=2),
                op=ALU.mult,
            )

        def quant(s, src, codes, scales):
            c, g = units[s]
            cols = slice(CW * c, CW * (c + 1))
            nc.vector.quantize_mx(
                out=codes[:, g, cols].bitcast(FP8X4),
                scales=scales[:, g, cols],
                in_=src[s][:].rearrange("p j t -> p (j t)"),
            )

        banks = [([i], 0, 512) for i in range(NC)]
        banks += [([i, i + 1], 512, 256) for i in range(0, NC, 2)]
        banks += [(list(range(i, i + 4)), 768, 128) for i in (0, 4)]
        banks += [([i, i + 1], 896, 128) for i in range(0, NC, 2)]
        parts = []
        for b, (tiles, j0, n) in enumerate(banks):
            for k, i in enumerate(tiles):
                f_ready = last[(j0 + n - 1) // CW] + 4
                if j0 == 0 and i >= NC // 2:
                    for g in range(NG):
                        parts.append((max(units.index((i, g)) + 3, f_ready), b, k, (g,)))
                else:
                    parts.append((max(last[i] + 3, f_ready), b, k, tuple(range(NG))))
        parts.sort()
        acc = {}
        left = [sum(1 for part in parts if part[1] == b) for b in range(len(banks))]

        def s2(b, k, groups):
            tiles, j0, n = banks[b]
            if b not in acc:
                pool, tag = (ps_s1, "s1") if j0 == 896 else (ps_acc, "acc")
                acc[b] = pool.tile([P, len(tiles), n], F32, name=tag)
            i = tiles[k]
            for g in groups:
                nc.tensor.matmul_mx(
                    out=acc[b][:, k, :],
                    lhsT=uco[:, g, CW * i : CW * (i + 1)].bitcast(FP8X4),
                    lhsT_scale=usc[:, g, CW * i : CW * (i + 1)],
                    rhs=fco[:, g, j0 : j0 + n].bitcast(FP8X4),
                    rhs_scale=fsc[:, g, j0 : j0 + n],
                    start=(g == 0),
                    stop=(g == NG - 1),
                )

        rb = [keep.tile([P, NC, 512], BF16, name="rb%d" % h, align_bytes=64) for h in range(2)]
        pco = [keep.tile([P, D], U32, name="pco%d" % h, align_bytes=64) for h in range(2)]
        psc = [keep.tile([P, D], U8, name="psc%d" % h, align_bytes=64) for h in range(2)]
        ot, pbank, pg = {}, {}, {}
        count = [0]

        def evac(b, tail):
            tiles, j0, n = banks[b]
            ot[b] = op.tile([P, len(tiles), n], F32, name="o")
            count[0] += 1
            if tail and count[0] % 2:
                nc.vector.tensor_scalar(
                    out=ot[b][:], in0=acc[b][:], scalar1=1.0 / ROOT_N, scalar2=None, op0=ALU.mult
                )
            else:
                nc.scalar.activation(out=ot[b][:], in_=acc[b][:], func=ACT.Copy, scale=1.0 / ROOT_N)

        def finish(b):
            tiles, j0, n = banks[b]
            for k, i in enumerate(tiles):
                d0 = CW * i - j0
                if 0 <= d0 < n:
                    blk = ot[b][:, k, d0 : d0 + CW]
                    nc.vector.tensor_tensor(out=blk, in0=blk, in1=neg_eye[:], op=ALU.add)

        def cast(b):
            tiles, j0, n = banks[b]
            h, c0 = j0 // 512, j0 % 512
            nc.sync.dma_start(
                out=grad[P * tiles[0] : P * (tiles[-1] + 1), j0 : j0 + n].rearrange("(k p) j -> p k j", p=P),
                in_=ot[b][:],
            )
            nc.vector.tensor_copy(out=rb[h][:, tiles[0] : tiles[-1] + 1, c0 : c0 + n], in_=ot[b][:])

        def p_transpose(h, i):
            pbank[h, i] = ps_tr.tile([P, 2, 2, P], F32, name="tr")
            for k in range(2):
                words = rb[h][:, i + k, :].bitcast(F32)
                for u in range(2):
                    nc.tensor.transpose(pbank[h, i][:, k, u, :], words[:, u::2], ident[:])

        def p_copy(h, i, tail):
            pg[h, i] = pp.tile([P, 2 * P, T], BF16, name="pg", align_bytes=64)
            dst = pg[h, i][:].rearrange("p m t -> p (m t)").bitcast(F32).rearrange("p (k m u) -> p k m u", k=2, u=2)
            src = pbank[h, i][:].rearrange("p k u m -> p k m u")
            if tail and i % 4 == 0:
                nc.vector.tensor_copy(out=dst, in_=src)
            else:
                nc.scalar.copy(out=dst, in_=src)

        def p_quant(h, i):
            cols = slice(P * i, P * (i + 2))
            nc.vector.quantize_mx(
                out=pco[h][:, cols].bitcast(FP8X4),
                scales=psc[h][:, cols],
                in_=pg[h, i][:].rearrange("p m t -> p (m t)"),
            )
            if i % 4 == 2:
                m0 = P * (i - 2)
                nc.sync.dma_start(
                    out=grad_words[h].rearrange("p m t -> p (m t)")[:, 4 * m0 : 4 * (m0 + 512)].bitcast(I32),
                    in_=pco[h][:, m0 : m0 + 512].bitcast(I32),
                )
            if i == NC - 2:
                for q in range(4):
                    nc.sync.dma_start(
                        out=grad_scales[h, 4 * q : 4 * q + 4, :].bitcast(I32),
                        in_=psc[h][32 * q : 32 * q + 4, :].bitcast(I32),
                    )

        for g in range(RA_HEAD):
            for t in range(T):
                make_ra(0, g, t, "V")
        later = [(half, g, t) for half in range(2) for g in range(NG) for t in range(T)][T * RA_HEAD :]
        ra_at = {}
        for m, item in enumerate(later):
            ra_at.setdefault(RA_FIRST + m * RA_STEP[0] // RA_STEP[1], []).append(item + (RA_ENGINE[m % len(RA_ENGINE)],))
        nc.vector.tensor_scalar(out=neg_eye[:], in0=ident[:], scalar1=-ROOT_N, scalar2=None, op0=ALU.mult)
        for j in (0, 2, 1, 3):
            x_transpose(j)
            x_copy(j)
        x_quant(0, 0)
        x_quant(0, 1)
        x_at, xc_at, xq_at = {}, {}, {}
        for j in range(4, 4 * NG):
            lead = 6 if j < 8 else X_LEAD
            x_at.setdefault(max(0, j - lead), []).append(j)
            xc_at.setdefault(max(1, j - lead + 1), []).append(j)
            if j % 2 == 1:
                xq_at.setdefault(max(2, j - lead + 2), []).append((j // 4, j % 4 // 2))
        s1(0)

        to_evac, to_finish, to_cast, to_copy, to_quant = [], [], [], [], []
        cast_left = [[sum(1 for tiles, j0, n in banks if j0 // 512 == h and i in tiles) for i in range(NC)] for h in range(2)]
        to_trans = []
        total = len(units)
        s = 0
        while s < total + 4 or parts or to_evac or to_finish or to_cast or to_trans or to_copy or to_quant:
            tail = s >= total + 2
            if s == 1:
                load_x(3, 2)
                load_w(512, 1024)
            if s < total:
                z_mul(s)
            for g, h in xq_at.get(s, []):
                x_quant(g, h)
            if s + 1 < total:
                s1(s + 1)
            for j in xc_at.get(s, []):
                x_copy(j)
            for j in x_at.get(s, []):
                x_transpose(j)
            if 1 <= s <= total:
                u_copy(s - 1)
                tanh(s - 1)
            if 2 <= s < total + 2:
                quant(s - 2, ub, uco, usc)
                f_mul(s - 2)
            if 3 <= s < total + 3:
                quant(s - 3, fb, fco, fsc)
            for item in ra_at.get(s, []):
                make_ra(*item)
            for h, i in to_quant:
                p_quant(h, i)
            to_quant = []
            for h, i in to_copy:
                p_copy(h, i, tail)
                to_quant.append((h, i))
            to_copy = []
            for h, i in to_trans[:2]:
                p_transpose(h, i)
                to_copy.append((h, i))
            to_trans = to_trans[2:]
            for b in to_cast:
                cast(b)
                tiles, j0, n = banks[b]
                h = j0 // 512
                for i in tiles:
                    cast_left[h][i] -= 1
                for i in tiles:
                    pair = i - i % 2
                    if cast_left[h][pair] == 0 and cast_left[h][pair + 1] == 0 and (h, pair) not in to_trans:
                        to_trans.append((h, pair))
            to_cast = []
            for b in to_finish:
                finish(b)
                to_cast.append(b)
            to_finish = []
            for b in to_evac:
                evac(b, tail)
                to_finish.append(b)
            to_evac = []
            cols = 0
            while parts and parts[0][0] <= s and cols < PART_COLS * (2 if tail else 1):
                ready, b, k, groups = parts.pop(0)
                s2(b, k, groups)
                cols += banks[b][2] * len(groups)
                left[b] -= 1
                if left[b] == 0:
                    to_evac.append(b)
            s += 1
